import numpy as np
import ml_dtypes


def mxq(x, axis, fmt="e4m3"):
    dtype, down = {"e4m3": (ml_dtypes.float8_e4m3fn, 7), "e5m2": (ml_dtypes.float8_e5m2, 14)}[fmt]
    v = np.moveaxis(np.asarray(x, np.float32).astype(ml_dtypes.bfloat16).astype(np.float64), axis, -1)
    blocks = v.reshape(v.shape[:-1] + (-1, 32))
    amax = np.abs(blocks).max(-1, keepdims=True)
    byte = np.maximum(np.where(amax > 0, np.frexp(amax)[1] - 1 + 127, 0) - down, 1)
    scale = np.exp2(byte - 127.0)
    codes = (blocks / scale).astype(np.float32).astype(dtype).astype(np.float64)
    return np.moveaxis((codes * scale).reshape(v.shape), -1, axis)


WIDE = False


def mx_kscale(k):
    if not WIDE:
        return np.ones(k)
    levels = np.array([10, -10, 5, -5, 0])
    if k % 512:
        return np.exp2(np.random.permutation(np.resize(levels, k // 32))).repeat(32)
    a = np.empty((k // 512, 16))
    for p in range(k // 512):
        a[p, :8] = np.random.permutation(np.resize(levels, 8))
        for g in range(8):
            far = levels[np.abs(levels - a[p, g]) >= 10]
            a[p, g + 8] = far[np.random.randint(len(far))]
    return np.exp2(a.ravel()).repeat(32)


def f64(x):
    return np.asarray(x).astype(np.float64)


def striped(idx):
    return np.tile(idx.reshape(-1, 16).T, (8, 1)).astype(np.uint16)


def unstriped(offs):
    return offs[:16].T.reshape(-1).astype(np.int64)


E2M1 = np.array([0.0, 0.5, 1.0, 1.5, 2.0, 3.0, 4.0, 6.0, -0.0, -0.5, -1.0, -1.5, -2.0, -3.0, -4.0, -6.0])


def pack_weight(w, fmt):
    k, n = w.shape
    w = f64(np.asarray(w, np.float32).astype(ml_dtypes.bfloat16)).reshape(k // 32, 32, n)
    amax = np.abs(w).max(1)
    if fmt == "e4m3":
        byte = np.frexp(amax)[1] - 1 + 127 - 7
    else:
        mant, ex = np.frexp(amax / 6.0)
        byte = np.where(mant > 0.5, ex, ex - 1) + 127
    byte = np.clip(np.where(amax > 0, byte, 1), 1, 254)
    scaled = (w * np.exp2(127.0 - byte)[:, None, :]).reshape(k, n).astype(np.float32)
    by_word = np.ascontiguousarray(scaled.reshape(k // 512, 128, 4, n).transpose(0, 1, 3, 2))
    if fmt == "e4m3":
        words = by_word.astype(ml_dtypes.float8_e4m3fn).view(np.uint8)
    else:
        c = by_word.astype(ml_dtypes.float4_e2m1fn).view(np.uint8) & 0xF
        words = (c[..., 0::2] | (c[..., 1::2] << 4)).reshape(k // 512, 128, 2 * n)
    return np.ascontiguousarray(words), np.ascontiguousarray(byte.astype(np.uint8).reshape(k // 512, 16, n))


def unpack_weight(words, scales, fmt):
    g, _, n = scales.shape
    words = np.ascontiguousarray(words).reshape(g, 128, n, -1)
    if fmt == "e4m3":
        vals = words.view(ml_dtypes.float8_e4m3fn).astype(np.float64)
    else:
        nib = np.empty((g, 128, n, 4), np.uint8)
        nib[..., 0::2] = words & 0xF
        nib[..., 1::2] = words >> 4
        vals = E2M1[nib]
    vals = vals * np.repeat(np.exp2(scales.astype(np.float64) - 127.0), 8, axis=1)[..., None]
    return vals.transpose(0, 1, 3, 2).reshape(g * 512, n)


def gelu(v):
    return 0.5 * v * (1.0 + np.tanh(np.sqrt(2.0 / np.pi) * (v + 0.044715 * v**3)))


def bf(x):
    return np.asarray(x, np.float32).astype(ml_dtypes.bfloat16)


def planes(Y):
    n, m = Y.shape
    b = f64(bf(Y)).reshape(n // 32, 32, m)
    amax = np.abs(b).max(1)
    byte = np.clip(np.where(amax > 0, np.frexp(amax)[1] - 1 + 127 - 7, 1), 1, 254)
    codes = (b * np.exp2(127.0 - byte)[:, None, :]).reshape(n, m).astype(np.float32).astype(ml_dtypes.float8_e4m3fn).view(np.uint8)
    words = codes.reshape(n // 512, 128, 4, m).transpose(0, 1, 3, 2)
    return np.ascontiguousarray(words), np.ascontiguousarray(byte.astype(np.uint8).reshape(n // 512, 16, m))


K, T, S, H, P, P2 = 1536, 2048, 1024, 1024, 512, 256

def setup_inputs():
    n = np.random.standard_normal
    s = mx_kscale(K)[:, None]
    u = mx_kscale(H)[:, None]
    tab_words, tab_scales = pack_weight(n((K, T)) * s, "e4m3")
    w1 = 1.5 * n((K, H)) / np.sqrt(K) / s
    gain = np.exp(0.3 * n(H)) * u[:, 0]
    size = np.exp(0.8 * n(H))
    w4 = 0.4 * n((H, H)) / np.sqrt(H) / u * size[None, :]
    w4_words, w4_scales = pack_weight(w4, "e2m1")
    res = np.random.uniform(0.25, 0.5, H) * size / u[:, 0]
    return {
        "tab_words": tab_words, "tab_scales": tab_scales,
        "offs": striped(np.random.permutation(T)[:S]),
        "w1": w1.astype(np.float32),
        "gain": gain.astype(np.float32),
        "pos1": striped(np.random.permutation(S)[:P]),
        "pos2": striped(np.random.permutation(S)[:P]),
        "w4_words": w4_words, "w4_scales": w4_scales,
        "res": res.astype(np.float32),
        "pos3": striped(np.random.permutation(P)[:P2]),
        "pos4": striped(np.random.permutation(P)[:P2]),
    }

def reference(tab_words, tab_scales, offs, w1, gain, pos1, pos2, w4_words, w4_scales, res, pos3, pos4):
    v = unpack_weight(tab_words, tab_scales, "e4m3")[:, unstriped(offs)]
    a = mxq(f64(w1), 0, "e4m3").T @ v
    h = a / (1 + np.exp(-a)) * f64(gain)[:, None]
    x = np.maximum(h[:, unstriped(pos1)], h[:, unstriped(pos2)])
    w4 = unpack_weight(w4_words, w4_scales, "e2m1")
    load = (w4.T @ mxq(x, 0, "e4m3")) + f64(res)[:, None] * x
    y = load[:, unstriped(pos3)] * np.tanh(load[:, unstriped(pos4)])
    words, scales = planes(y)
    return y, words, scales

from contextlib import ExitStack

import concourse.mybir as mybir

K, T, S, H, PAIRS, FACING = 1536, 2048, 1024, 1024, 512, 256
FLOPS = 2 * K * H * S + 2 * H * H * PAIRS

F32 = mybir.dt.float32
BF16 = mybir.dt.bfloat16
I32 = mybir.dt.int32
U32 = mybir.dt.uint32
U16 = mybir.dt.uint16
U8 = mybir.dt.uint8
FP8X4 = mybir.dt.float8_e4m3fn_x4
FP4X4 = mybir.dt.float4_e2m1fn_x4
ACT = mybir.ActivationFunctionType
ALU = mybir.AluOpType

P = 128
PACK = 4
K_PASS = P * PACK
K_PASSES = K // K_PASS
GROUPS = H // K_PASS
BANK = 512
HALF = PAIRS // 2


def tile_list_truss_load_features_kernel(
    tc, tab_words, tab_scales, offs, w1, gain, pos1, pos2, w4_words, w4_scales, res, pos3, pos4, out_0, out_1, out_2
):
    nc = tc.nc
    with ExitStack() as ctx:
        keep = ctx.enter_context(tc.tile_pool(name="keep", bufs=1))
        ring = ctx.enter_context(tc.tile_pool(name="ring", bufs=2))
        psum = ctx.enter_context(tc.psum_pool(name="psum", bufs=1))

        def load_list(name, src):
            tile = keep.tile(list(src.shape), U16, name=name)
            nc.sync.dma_start(tile[:], src)
            return tile

        def load_table_words(a):
            tile = keep.tile([P, T], I32, name=f"tab_words{a}")
            nc.sync.dma_start(tile[:], tab_words[a].rearrange("p t i -> p (t i)").bitcast(I32))
            return tile

        def load_w1(a, b, lo=0, hi=K_PASS):
            raw = ring.tile([P, PACK, hi - lo], F32, name=f"w1_raw{hi - lo}", bufs=4 if hi - lo < K_PASS else 3)
            rows = w1[a * K_PASS : (a + 1) * K_PASS, b * K_PASS + lo : b * K_PASS + hi]
            nc.sync.dma_start(raw[:], rows.rearrange("(p j) c -> p j c", j=PACK))
            return raw

        def gather_words(a):
            picked = keep.tile([P, S], U32, name=f"picked_words{a}", align_bytes=64)
            nc.vector.tensor_copy(picked[:], tab_tiles[a][:].bitcast(U32).indirect(offs_t[:]))
            return picked

        def round_w1(parts, name="w1_bf16"):
            rounded = ring.tile([P, PACK * K_PASS], BF16, name=name, bufs=2 if name == "w1_bf16" else 1, align_bytes=64)
            dst = rounded[:].rearrange("p (t m j) -> p m j t", t=PACK, j=PACK)
            m0 = 0
            for engine_copy, raw in parts:
                src = raw[:].rearrange("p j (m t) -> p m j t", t=PACK)
                engine_copy(dst[:, m0 : m0 + src.shape[1]], src)
                m0 = m0 + src.shape[1]
            return rounded

        def quantise(name, rounded, width):
            codes = keep.tile([P, width], U32, name=name + "_codes", align_bytes=64)
            scales = keep.tile([P, width], U8, name=name + "_scales", align_bytes=64)
            nc.vector.quantize_mx(out=codes[:].bitcast(FP8X4), scales=scales[:], in_=rounded)
            return codes, scales

        def bank(i):
            return psum.tile([P, BANK], F32, name=f"bank{i}")

        def interleave(engine_copy, name, src, width):
            dst = keep.tile([P, width * PACK], BF16, name=name, align_bytes=64)
            engine_copy(
                dst[:].rearrange("p (c i t) -> p c t i", i=4, t=PACK),
                src.rearrange("p t (c i) -> p c t i", i=4),
            )
            return dst

        tab_planes = keep.tile([P, T], U8, name="tab_planes")
        w4_planes = keep.tile([P, H], U8, name="w4_planes")
        nc.vector.memset(tab_planes[:].bitcast(I32), 0)
        nc.vector.memset(w4_planes[:].bitcast(I32), 0)

        gain_t = keep.tile([P, GROUPS, PACK], F32, name="gain_t")
        res_t = keep.tile([P, GROUPS, PACK], F32, name="res_t")
        nc.gpsimd.dma_start(gain_t[:], gain.rearrange("(g p t) -> p g t", p=P, t=PACK))
        nc.gpsimd.dma_start(res_t[:], res.rearrange("(g p t) -> p g t", p=P, t=PACK))

        half = K_PASS // 2
        tab_tiles = [load_table_words(0)]
        offs_t = load_list("offs_t", offs)
        first_half = load_w1(0, 0, 0, half)
        for q in range(4):
            nc.sync.dma_start(
                tab_planes[32 * q : 32 * q + 4 * K_PASSES, :].bitcast(I32),
                tab_scales[:, 4 * q : 4 * q + 4, :].bitcast(I32),
            )
        raws = {(0, 0): [(nc.scalar.copy, first_half), (nc.scalar.copy, load_w1(0, 0, half, K_PASS))]}
        tab_tiles.append(load_table_words(1))
        raws[(1, 0)] = [(nc.scalar.copy, load_w1(1, 0, 0, half)), (nc.scalar.copy, load_w1(1, 0, half, K_PASS))]
        tab_tiles.append(load_table_words(2))
        raws[(2, 0)] = [(nc.scalar.copy, load_w1(2, 0, 0, half)), (nc.vector.tensor_copy, load_w1(2, 0, half, K_PASS))]
        pos1_t = load_list("pos1_t", pos1)
        pos2_t = load_list("pos2_t", pos2)
        w4_raw = keep.tile([P, GROUPS, 2 * H], U8, name="w4_raw")
        nc.sync.dma_start(w4_raw[:].bitcast(I32), w4_words.rearrange("a p c -> p a c").bitcast(I32))
        for q in range(4):
            nc.sync.dma_start(
                w4_planes[32 * q : 32 * q + 4 * GROUPS, :].bitcast(I32),
                w4_scales[:, 4 * q : 4 * q + 4, :].bitcast(I32),
            )

        picked = []
        w1_mx = {}
        picked_planes = keep.tile([P, S], U8, name="picked_planes", align_bytes=64)
        for a in range(K_PASSES):
            picked.append(gather_words(a))
            if a == 0:
                nc.vector.tensor_copy(picked_planes[:], tab_planes[:].indirect(offs_t[:]))
            rounded = round_w1(raws[(a, 0)], "before_w4" if a == K_PASSES - 1 else "w1_bf16")
            w1_mx[(a, 0)] = quantise(f"w1_{a}_0", rounded[:], K_PASS)

        for a in range(K_PASSES):
            engine_copy = nc.vector.tensor_copy if a == K_PASSES - 1 else nc.scalar.copy
            raws[(a, 1)] = [(engine_copy, load_w1(a, 1))]
        pos3_t = load_list("pos3_t", pos3)
        pos4_t = load_list("pos4_t", pos4)

        def first_product(b):
            banks = [bank(i) for i in range(8)]
            for t in range(PACK):
                for a in range(K_PASSES):
                    codes, scales = w1_mx[(a, b)]
                    for hf in range(2):
                        cols = slice(hf * BANK, (hf + 1) * BANK)
                        nc.tensor.matmul_mx(
                            out=banks[2 * t + hf][:],
                            lhsT=codes[:, t * P : (t + 1) * P].bitcast(FP8X4),
                            lhsT_scale=scales[:, t * P : (t + 1) * P],
                            rhs=picked[a][:, cols].bitcast(FP8X4),
                            rhs_scale=picked_planes[4 * a : P, cols],
                            start=(a == 0),
                            stop=(a == K_PASSES - 1),
                        )
            return banks

        def silu(banks, t):
            act = ring.tile([P, S], F32, name="act", bufs=5)
            for hf in range(2):
                nc.scalar.activation(act[:, hf * BANK : (hf + 1) * BANK], banks[2 * t + hf][:], ACT.Silu)
            return act

        def apply_gain(act, b, t):
            nc.scalar.activation(act[:], act[:], ACT.Copy, scale=gain_t[:, b, t : t + 1])

        def join_gained_pairs(hs, x, t0, lo, hi):
            width = hi - lo
            first = ring.tile([P, len(hs), width], F32, name="first")
            second = ring.tile([P, len(hs), width], F32, name="second")
            for u, h in enumerate(hs):
                nc.vector.tensor_copy(first[:, u, :], h[:].indirect(pos1_t[:, lo // 16 : hi // 16]))
                nc.vector.tensor_copy(second[:, u, :], h[:].indirect(pos2_t[:, lo // 16 : hi // 16]))
            nc.vector.tensor_tensor(x[:, t0 : t0 + len(hs), lo:hi], second[:], first[:], ALU.max)

        def join_pairs(act, x, b, t, lo, hi):
            width = hi - lo
            first = ring.tile([P, PAIRS], F32, name="first")
            second = ring.tile([P, PAIRS], F32, name="second")
            first_gained = ring.tile([P, PAIRS], F32, name="first_gained", bufs=1)
            g = gain_t[:, b, t : t + 1]
            nc.vector.tensor_copy(first[:, :width], act[:].indirect(pos1_t[:, lo // 16 : hi // 16]))
            nc.scalar.activation(first_gained[:, :width], first[:, :width], ACT.Copy, scale=g)
            nc.vector.tensor_copy(second[:, :width], act[:].indirect(pos2_t[:, lo // 16 : hi // 16]))
            nc.vector.scalar_tensor_tensor(
                x[:, t, lo:hi], second[:, :width], g, first_gained[:, :width], ALU.mult, ALU.max
            )

        xs = [keep.tile([P, PACK, PAIRS], F32, name=f"x{b}") for b in range(GROUPS)]
        x_mx = {}

        banks = first_product(0)
        w4_dealt = ring.tile([P, GROUPS, 2 * H], U8, name="w4_dealt", tag="before_w4", bufs=1, align_bytes=64)
        nc.vector.tensor_copy(
            w4_dealt[:].rearrange("p a c -> p (a c)").bitcast(U16).rearrange("p (g t m) -> p g m t", t=PACK, m=P),
            w4_raw[:].rearrange("p a c -> p (a c)").bitcast(U16).rearrange("p (g m t) -> p g m t", t=PACK, m=P),
        )
        w4_plane = [keep.tile([P, H], U8, name=f"w4_plane{a}", align_bytes=64) for a in range(GROUPS)]
        nc.vector.tensor_copy(
            w4_plane[0][:].rearrange("p (g t m) -> p g m t", t=PACK, m=P),
            w4_planes[:].rearrange("p (g m t) -> p g m t", t=PACK, m=P),
        )
        for q in range(4):
            nc.sync.dma_start(
                w4_plane[1][32 * q : 32 * q + 4, :].bitcast(I32),
                w4_plane[0][32 * q + 4 : 32 * q + 8, :].bitcast(I32),
            )
        acts = [silu(banks, 0), silu(banks, 1)]
        join_pairs(acts[0], xs[0], 0, 0, 0, PAIRS)
        apply_gain(acts[1], 0, 1)
        acts.append(silu(banks, 2))
        apply_gain(acts[2], 0, 2)
        join_gained_pairs(acts[1:3], xs[0], 1, 0, PAIRS)
        for a in range(K_PASSES):
            rounded = round_w1(raws[(a, 1)])
            w1_mx[(a, 1)] = quantise(f"w1_{a}_1", rounded[:], K_PASS)
        acts.append(silu(banks, 3))
        apply_gain(acts[3], 0, 3)
        join_gained_pairs(acts[3:], xs[0], 3, 0, PAIRS)

        banks = first_product(1)
        acts = [silu(banks, 0), silu(banks, 1)]
        join_pairs(acts[0], xs[1], 1, 0, 0, PAIRS)
        apply_gain(acts[1], 1, 1)
        for t in (2, 3):
            acts.append(silu(banks, t))
            apply_gain(acts[t], 1, t)
        join_gained_pairs(acts[1:3], xs[1], 1, 0, PAIRS)
        for hf in range(2):
            xb = interleave(nc.scalar.copy, f"xb0_{hf}", xs[0][:, :, hf * HALF : (hf + 1) * HALF], HALF)
            x_mx[(0, hf)] = quantise(f"x0_{hf}", xb[:], HALF)

        def second_product(hf):
            out_banks = []
            for i in range(4):
                acc = bank(4 * hf + i)
                for u in range(2):
                    s = 2 * i + u
                    for a in range(GROUPS):
                        codes, scales = x_mx[(a, hf)]
                        nc.tensor.matmul_mx(
                            out=acc[:, u * HALF : (u + 1) * HALF],
                            lhsT=w4_dealt[:, a, 2 * P * s : 2 * P * (s + 1)].bitcast(FP4X4),
                            lhsT_scale=w4_plane[a][:, s * P : (s + 1) * P],
                            rhs=codes[:].bitcast(FP8X4),
                            rhs_scale=scales[:],
                            start=(a == 0),
                            stop=(a == GROUPS - 1),
                        )
                out_banks.append(acc)
            return out_banks

        loads = [keep.tile([P, PAIRS], F32, name=f"load{s}") for s in range(GROUPS * PACK)]

        def residual(accs, s, hf):
            g, t = divmod(s, PACK)
            cols = slice(hf * HALF, (hf + 1) * HALF)
            nc.vector.scalar_tensor_tensor(
                loads[s][:, cols],
                xs[g][:, t, cols],
                res_t[:, g, t : t + 1],
                accs[s // 2][:, (s % 2) * HALF : (s % 2 + 1) * HALF],
                ALU.mult,
                ALU.add,
            )

        accs = []
        join_gained_pairs(acts[3:], xs[1], PACK - 1, 0, HALF)
        xb_lo = interleave(nc.scalar.copy, "xb1_0", xs[1][:, :, :HALF], HALF)
        join_gained_pairs(acts[3:], xs[1], PACK - 1, HALF, PAIRS)
        xb_hi = interleave(nc.scalar.copy, "xb1_1", xs[1][:, :, HALF:], HALF)
        x_mx[(1, 0)] = quantise("x1_0", xb_lo[:], HALF)
        accs.append(second_product(0))
        for s in range(4):
            residual(accs[0], s, 0)
        x_mx[(1, 1)] = quantise("x1_1", xb_hi[:], HALF)
        accs.append(second_product(1))
        for s in range(4, 8):
            residual(accs[0], s, 0)

        y_scales = keep.tile([P, GROUPS, FACING], U8, name="y_scales", align_bytes=64)
        y_rows = out_0.rearrange("(g p t) m -> g p t m", p=P, t=PACK)
        ys = [keep.tile([P, PACK, FACING], F32, name=f"y{g}") for g in range(GROUPS)]
        tanhs = {}

        def other_side(s):
            residual(accs[1], s, 1)
            other = ring.tile([P, FACING], F32, name="other")
            nc.vector.tensor_copy(other[:], loads[s][:].indirect(pos4_t[:]))
            squashed = ring.tile([P, FACING], F32, name="squashed", bufs=3)
            nc.scalar.activation(squashed[:], other[:], ACT.Tanh)
            tanhs[s] = squashed

        def finish_group(g, engine_copy):
            yb = interleave(engine_copy, f"yb{g}", ys[g][:], FACING)
            codes = keep.tile([P, FACING], I32, name=f"y_codes{g}", align_bytes=64)
            nc.vector.quantize_mx(out=codes[:].bitcast(FP8X4), scales=y_scales[:, g, :], in_=yb[:])
            nc.sync.dma_start(out_1[g].rearrange("p m t -> p (m t)").bitcast(I32), codes[:])

        other_side(0)
        for s in range(GROUPS * PACK):
            g, t = divmod(s, PACK)
            if s + 1 < GROUPS * PACK:
                other_side(s + 1)
            nc.vector.tensor_tensor(ys[g][:, t, :], loads[s][:].indirect(pos3_t[:]), tanhs[s][:], ALU.mult)
            nc.sync.dma_start(y_rows[g][:, t, :], ys[g][:, t, :])
            if s == PACK:
                finish_group(0, nc.scalar.copy)
        finish_group(1, nc.vector.tensor_copy)
        for q in range(4):
            queue = nc.scalar if q % 2 else nc.sync
            queue.dma_start(
                out_2[:, 4 * q : 4 * q + 4, :].rearrange("g r m -> r g m").bitcast(I32),
                y_scales[32 * q : 32 * q + 4].bitcast(I32),
            )
